import numpy as np
import ml_dtypes


def mxq(x, axis, fmt="e4m3"):
    dtype, down = {"e4m3": (ml_dtypes.float8_e4m3fn, 7), "e5m2": (ml_dtypes.float8_e5m2, 14)}[fmt]
    v = np.moveaxis(np.asarray(x, np.float32).astype(ml_dtypes.bfloat16).astype(np.float64), axis, -1)
    blocks = v.reshape(v.shape[:-1] + (-1, 32))
    amax = np.abs(blocks).max(-1, keepdims=True)
    byte = np.maximum(np.where(amax > 0, np.frexp(amax)[1] - 1 + 127, 0) - down, 1)
    scale = np.exp2(byte - 127.0)
    codes = (blocks / scale).astype(np.float32).astype(dtype).astype(np.float64)
    return np.moveaxis((codes * scale).reshape(v.shape), -1, axis)


WIDE = False


def mx_kscale(k):
    if not WIDE:
        return np.ones(k)
    levels = np.array([10, -10, 5, -5, 0])
    if k % 512:
        return np.exp2(np.random.permutation(np.resize(levels, k // 32))).repeat(32)
    a = np.empty((k // 512, 16))
    for p in range(k // 512):
        a[p, :8] = np.random.permutation(np.resize(levels, 8))
        for g in range(8):
            far = levels[np.abs(levels - a[p, g]) >= 10]
            a[p, g + 8] = far[np.random.randint(len(far))]
    return np.exp2(a.ravel()).repeat(32)


def f64(x):
    return np.asarray(x).astype(np.float64)


def striped(idx):
    return np.tile(np.asarray(idx).reshape(-1, 16).T, (8, 1)).astype(np.uint16)


def unstriped(offs):
    return offs[:16].T.reshape(-1).astype(np.int64)


E2M1 = np.array([0.0, 0.5, 1.0, 1.5, 2.0, 3.0, 4.0, 6.0, -0.0, -0.5, -1.0, -1.5, -2.0, -3.0, -4.0, -6.0])


def pack_weight(w, fmt):
    k, n = w.shape
    w = f64(np.asarray(w, np.float32).astype(ml_dtypes.bfloat16)).reshape(k // 32, 32, n)
    amax = np.abs(w).max(1)
    if fmt == "e4m3":
        byte = np.frexp(amax)[1] - 1 + 127 - 7
    else:
        mant, ex = np.frexp(amax / 6.0)
        byte = np.where(mant > 0.5, ex, ex - 1) + 127
    byte = np.clip(np.where(amax > 0, byte, 1), 1, 254)
    scaled = (w * np.exp2(127.0 - byte)[:, None, :]).reshape(k, n).astype(np.float32)
    by_word = np.ascontiguousarray(scaled.reshape(k // 512, 128, 4, n).transpose(0, 1, 3, 2))
    if fmt == "e4m3":
        words = by_word.astype(ml_dtypes.float8_e4m3fn).view(np.uint8)
    else:
        c = by_word.astype(ml_dtypes.float4_e2m1fn).view(np.uint8) & 0xF
        words = (c[..., 0::2] | (c[..., 1::2] << 4)).reshape(k // 512, 128, 2 * n)
    return np.ascontiguousarray(words), np.ascontiguousarray(byte.astype(np.uint8).reshape(k // 512, 16, n))


def unpack_weight(words, scales, fmt):
    g, _, n = scales.shape
    words = np.ascontiguousarray(words).reshape(g, 128, n, -1)
    if fmt == "e4m3":
        vals = words.view(ml_dtypes.float8_e4m3fn).astype(np.float64)
    else:
        nib = np.empty((g, 128, n, 4), np.uint8)
        nib[..., 0::2] = words & 0xF
        nib[..., 1::2] = words >> 4
        vals = E2M1[nib]
    vals = vals * np.repeat(np.exp2(scales.astype(np.float64) - 127.0), 8, axis=1)[..., None]
    return vals.transpose(0, 1, 3, 2).reshape(g * 512, n)


def sigmoid(v):
    return 1.0 / (1.0 + np.exp(-v))


def bf(x):
    return np.asarray(x, np.float32).astype(ml_dtypes.bfloat16)


def planes(Y):
    r, m = Y.shape
    b = f64(bf(Y)).reshape(r // 32, 32, m)
    amax = np.abs(b).max(1)
    byte = np.clip(np.where(amax > 0, np.frexp(amax)[1] - 1 + 127 - 7, 1), 1, 254)
    codes = (b * np.exp2(127.0 - byte)[:, None, :]).reshape(r, m).astype(np.float32).astype(ml_dtypes.float8_e4m3fn).view(np.uint8)
    words = codes.reshape(r // 512, 128, 4, m).transpose(0, 1, 3, 2)
    return np.ascontiguousarray(words), np.ascontiguousarray(byte.astype(np.uint8).reshape(r // 512, 16, m))


K, R, F, T, J, U = 512, 512, 512, 2048, 256, 512


def setup_inputs():
    n = np.random.standard_normal
    idx = np.random.permutation(T)[:J]
    idx2 = np.random.permutation(U)[:J]
    fk = mx_kscale(K)
    fr = mx_kscale(R)
    tabp = pack_weight(n((K, T)) / fk[:, None], "e2m1")
    dtabp = pack_weight(n((K, T)) / fk[:, None], "e2m1")
    return {
        "tab_words": tabp[0],
        "tab_scales": tabp[1],
        "dtab_words": dtabp[0],
        "dtab_scales": dtabp[1],
        "w1": (n((K, R)) * 1 / np.sqrt(K) * fk[:, None]).astype(np.float32),
        "w2": (n((K, R)) * 1.4 / np.sqrt(K) * fk[:, None]).astype(np.float32),
        "bias": (np.random.uniform(-0.5, 0.5, (R, 1))).astype(np.float32),
        "carry": (n((R, U)) * 0.7).astype(np.float32),
        "rs": (np.random.uniform(0.5, 2.0, (R, 1)) * fr[:, None]).astype(np.float32),
        "wor": (n((R, F)) * 1 / np.sqrt(R) / fr[:, None]).astype(np.float32),
        "res": (n((F, J)) * 0.5).astype(np.float32),
        "offs": striped(idx),
        "offs2": striped(idx2),
    }


def reference(tab_words, tab_scales, dtab_words, dtab_scales, w1, w2, bias, carry, rs, wor, res, offs, offs2):
    idx = unstriped(offs)
    idx2 = unstriped(offs2)
    tabu = unpack_weight(tab_words, tab_scales, "e2m1")
    dtabu = unpack_weight(dtab_words, dtab_scales, "e2m1")
    w1q = mxq(f64(w1), 0, "e4m3")
    tabidxg = tabu[:, idx]
    a = w1q.T @ tabidxg
    dtabidxg = dtabu[:, idx]
    ta = w1q.T @ dtabidxg
    w2q = mxq(f64(w2), 0, "e4m3")
    b = w2q.T @ tabidxg
    tb = w2q.T @ dtabidxg
    h1 = np.tanh(a)
    gt = sigmoid(b + f64(bias))
    th1 = ta * (1.0 - np.square(h1))
    tgt = tb * gt * (1.0 - gt)
    tu1 = th1 * gt + tgt * (h1 - f64(carry)[:, idx2])
    fo1 = tu1 * f64(rs)
    worq = mxq(f64(wor), 0, "e4m3")
    fo1q = mxq(fo1, 0, "e4m3")
    yo = worq.T @ fo1q
    y = yo + f64(res)
    words, scales = planes(y)
    return y, words, scales

@@ -1,0 +1,237 @@
+from contextlib import ExitStack
+
+import concourse.mybir as mybir
+
+K, R, F, T, J, U = 512, 512, 512, 2048, 256, 512
+FLOPS = 671088640
+
+F32 = mybir.dt.float32
+BF16 = mybir.dt.bfloat16
+I32 = mybir.dt.int32
+U32 = mybir.dt.uint32
+U16 = mybir.dt.uint16
+U8 = mybir.dt.uint8
+FP8X4 = mybir.dt.float8_e4m3fn_x4
+FP4X4 = mybir.dt.float4_e2m1fn_x4
+ALU = mybir.AluOpType
+ACT = mybir.ActivationFunctionType
+
+P = 128
+PACK = 4
+HALF = J // 2
+
+
+def tile_attend_tccarrymix_o_pl_kernel(tc, tab_words, tab_scales, dtab_words, dtab_scales, w1, w2, bias, carry, rs,
+                                        wor, res, offs, offs2, out_0, out_1, out_2):
+    nc = tc.nc
+    with ExitStack() as ctx:
+        sb = ctx.enter_context(tc.tile_pool(name="sb", bufs=1))
+        psum = ctx.enter_context(tc.psum_pool(name="psum", bufs=1))
+
+        def tile(name, shape, dtype):
+            return sb.tile(shape, dtype, name=name, align_bytes=64)
+
+        def bank(name, tag):
+            return psum.tile([P, PACK, HALF], F32, name=name, tag=tag)
+
+        idx = sb.tile([P, J // 16], U16, name="idx")
+        idx2 = sb.tile([P, J // 16], U16, name="idx2")
+        tab_sc = tile("tab_sc", [P, T], U8)
+        dtab_sc = tile("dtab_sc", [P, T], U8)
+        tab_w = tile("tab_w", [P, T], U16)
+        dtab_w = tile("dtab_w", [P, T], U16)
+        pieces = {"w1": 1, "w2": 2, "wor": 1}
+        raw = {n: [tile("raw_%s%d" % (n, c), [P, PACK, 512 // k], F32) for c in range(k)] for n, k in (("w1", 1), ("w2", 2), ("wor", 1))}
+        carry_t = [tile("carry%d" % t, [P, U], F32) for t in range(PACK)]
+        res_sb = tile("res_sb", [P, PACK, J], F32)
+        bias_sb = tile("bias_sb", [P, PACK], F32)
+        rs_sb = tile("rs_sb", [P, PACK], F32)
+
+        def load_scales(queue, dst, src):
+            rows = src[0].bitcast(I32).rearrange("(q i) c -> i q c", i=4)
+            for i in range(4):
+                queue.dma_start(out=dst[i:P:32, :].bitcast(I32), in_=rows[i])
+
+        def rows4(src):
+            return src.rearrange("(p t) c -> p t c", t=PACK)
+
+        nc.vector.memset(tab_sc[:].bitcast(I32), 0)
+        nc.vector.memset(dtab_sc[:].bitcast(I32), 0)
+        nc.sync.dma_start(idx[:], offs)
+        nc.sync.dma_start(out=raw["w1"][0][:], in_=rows4(w1))
+        load_scales(nc.sync, tab_sc, tab_scales)
+        nc.sync.dma_start(out=tab_w[:].bitcast(I32), in_=tab_words[0].bitcast(I32))
+        nc.sync.dma_start(out=dtab_w[:].bitcast(I32), in_=dtab_words[0].bitcast(I32))
+        load_scales(nc.sync, dtab_sc, dtab_scales)
+        for c in range(2):
+            nc.sync.dma_start(out=raw["w2"][c][:], in_=rows4(w2)[:, :, 256 * c:256 * (c + 1)])
+        nc.sync.dma_start(idx2[:], offs2)
+        nc.sync.dma_start(out=bias_sb[:], in_=bias.rearrange("(p t) o -> p (t o)", t=PACK))
+        nc.sync.dma_start(out=rs_sb[:], in_=rs.rearrange("(p t) o -> p (t o)", t=PACK))
+        for t in range(PACK):
+            nc.sync.dma_start(out=carry_t[t][:], in_=rows4(carry)[:, t, :])
+        nc.sync.dma_start(out=raw["wor"][0][:], in_=rows4(wor))
+        nc.sync.dma_start(out=res_sb[:], in_=rows4(res))
+
+        woven = {n: tile("woven_" + n, [P, PACK * 512], BF16) for n in raw}
+        codes = {n: tile("codes_" + n, [P, 512], U32) for n in raw}
+        scales = {n: tile("scales_" + n, [P, 512], U8) for n in raw}
+
+        def weave_weight(n, on_scalar, m0, m1):
+            dst = woven[n][:].rearrange("p (t m j) -> p m j t", t=PACK, j=PACK)[:, m0:m1]
+            per = P // pieces[n]
+            c = m0 // per
+            src = raw[n][c][:].rearrange("p j (m t) -> p m j t", t=PACK)[:, m0 - c * per:m1 - c * per]
+            if on_scalar:
+                nc.scalar.activation(out=dst, in_=src, func=ACT.Copy)
+            else:
+                nc.vector.tensor_copy(out=dst, in_=src)
+
+        def quantize_weight(n, t0, t1):
+            nc.vector.quantize_mx(out=codes[n][:, P * t0:P * t1].bitcast(FP8X4), scales=scales[n][:, P * t0:P * t1],
+                                  in_=woven[n][:, 512 * t0:512 * t1])
+
+        def gather(name, window, dtype):
+            got = tile(name, [P, J], dtype)
+            nc.vector.tensor_copy(out=got[:], in_=window[:].indirect(idx[:]))
+            return got
+
+        def product(dst, n, rhs, rhs_scale):
+            for t in range(PACK):
+                cols = slice(P * t, P * (t + 1))
+                nc.tensor.matmul_mx(out=dst[:, t, :], lhsT=codes[n][:, cols].bitcast(FP8X4), lhsT_scale=scales[n][:, cols],
+                                    rhs=rhs, rhs_scale=rhs_scale, start=True, stop=True)
+
+        halves = [slice(HALF * H, HALF * (H + 1)) for H in range(2)]
+
+        def first_layer(name, n, words, sc, H):
+            dst = bank("%s%d" % (name, H), "%s%d" % (name, H))
+            product(dst, n, words[:, halves[H]].bitcast(FP4X4), sc[:, halves[H]])
+            return dst
+
+        weave_weight("w1", True, 0, 64)
+        weave_weight("w1", False, 64, 128)
+        g_tab_sc = gather("g_tab_sc", tab_sc, U8)
+        for t in range(PACK):
+            quantize_weight("w1", t, t + 1)
+        g_tab_w = gather("g_tab_w", tab_w, U16)
+        a = [first_layer("a", "w1", g_tab_w, g_tab_sc, H) for H in range(2)]
+        g_dtab_w = gather("g_dtab_w", dtab_w, U16)
+        g_dtab_sc = gather("g_dtab_sc", dtab_sc, U8)
+        ta = [first_layer("ta", "w1", g_dtab_w, g_dtab_sc, H) for H in range(2)]
+
+        half_bias = tile("half_bias", [P, PACK], F32)
+        rs_quarter = tile("rs_quarter", [P, PACK], F32)
+        rs_neg_half = tile("rs_neg_half", [P, PACK], F32)
+        nc.gpsimd.tensor_scalar(out=half_bias[:], in0=bias_sb[:], scalar1=0.5, scalar2=0.0, op0=ALU.mult, op1=ALU.add)
+        nc.gpsimd.tensor_scalar(out=rs_quarter[:], in0=rs_sb[:], scalar1=0.25, scalar2=0.0, op0=ALU.mult, op1=ALU.add)
+        nc.gpsimd.tensor_scalar(out=rs_neg_half[:], in0=rs_sb[:], scalar1=-0.5, scalar2=0.0, op0=ALU.mult, op1=ALU.add)
+
+        h = tile("h", [P, PACK, J], F32)
+        hsq = tile("hsq", [P, PACK, J], F32)
+        u1 = tile("u1", [P, PACK, J], F32)
+        d = tile("d", [P, PACK, J], F32)
+        for H in range(2):
+            nc.scalar.activation(out=h[:, :, halves[H]], in_=a[H][:], func=ACT.Tanh)
+        for H in range(2):
+            nc.scalar.activation(out=hsq[:, :, halves[H]], in_=h[:, :, halves[H]], func=ACT.Square)
+
+        def th1(H):
+            nc.vector.scalar_tensor_tensor(out=u1[:, :, halves[H]], in0=hsq[:, :, halves[H]], scalar=1.0, in1=ta[H][:],
+                                           op0=ALU.subtract, op1=ALU.mult)
+
+        def carry_minus_h(t):
+            nc.vector.tensor_tensor(d[:, t, :], carry_t[t][:].indirect(idx2[:]), h[:, t, :], ALU.subtract)
+
+        weave_weight("w2", False, 0, 64)
+        weave_weight("w2", True, 64, 128)
+        th1(0)
+        th1(1)
+        carry_minus_h(0)
+        for t in range(PACK):
+            quantize_weight("w2", t, t + 1)
+        b, tb = [], []
+        for H in range(2):
+            b.append(first_layer("b", "w2", g_tab_w, g_tab_sc, H))
+            tb.append(first_layer("tb", "w2", g_dtab_w, g_dtab_sc, H))
+        for t in range(1, PACK):
+            carry_minus_h(t)
+        s = [tile("s%d" % H, [P, PACK, HALF], F32) for H in range(2)]
+        for H in range(2):
+            for t in range(PACK):
+                nc.scalar.activation(out=s[H][:, t, :], in_=b[H][:, t, :], func=ACT.Tanh, scale=0.5,
+                                     bias=half_bias[:, t:t + 1])
+        weave_weight("wor", True, 0, 128)
+
+        pairs = [slice(0, 2), slice(2, 4)]
+
+        def mix(H, between):
+            u2 = tile("u2_%d" % H, [P, PACK, HALF], F32)
+            u3 = tile("u3_%d" % H, [P, PACK, HALF], F32)
+            e = tile("e_%d" % H, [P, PACK, HALF], F32)
+            fo = tile("fo_%d" % H, [P, PACK, HALF], BF16)
+            for t in range(PACK):
+                nc.vector.scalar_tensor_tensor(out=u2[:, t, :], in0=tb[H][:, t, :], scalar=rs_quarter[:, t:t + 1],
+                                               in1=d[:, t, halves[H]], op0=ALU.mult, op1=ALU.mult)
+            for q in pairs:
+                nc.vector.scalar_tensor_tensor(out=u3[:, q, :], in0=s[H][:, q, :], scalar=1.0, in1=u2[:, q, :],
+                                               op0=ALU.subtract, op1=ALU.mult)
+            between()
+            for t in range(PACK):
+                nc.vector.scalar_tensor_tensor(out=e[:, t, :], in0=u1[:, t, halves[H]], scalar=rs_neg_half[:, t:t + 1],
+                                               in1=u3[:, t, :], op0=ALU.mult, op1=ALU.add)
+            for q in pairs:
+                nc.vector.scalar_tensor_tensor(out=fo[:, q, :], in0=s[H][:, q, :], scalar=1.0, in1=e[:, q, :],
+                                               op0=ALU.add, op1=ALU.mult)
+            return fo
+
+        def weave(name, src, on_scalar):
+            dst = tile(name, [P, HALF * PACK], BF16)
+            o = dst[:].rearrange("p (c i t) -> p c t i", i=4, t=PACK)
+            i = src[:].rearrange("p t (c i) -> p c t i", i=4)
+            if on_scalar:
+                nc.scalar.copy(out=o, in_=i)
+            else:
+                nc.vector.tensor_copy(out=o, in_=i)
+            return dst
+
+        y_codes = tile("y_codes", [P, J], U32)
+        y_scales = tile("y_scales", [P, J], U8)
+        words_out = out_1[0].rearrange("p c r -> p (c r)").bitcast(I32)
+
+        yo = {}
+
+        def last_layer(H, fo_woven):
+            f_codes = tile("f_codes%d" % H, [P, HALF], U32)
+            f_scales = tile("f_scales%d" % H, [P, HALF], U8)
+            nc.vector.quantize_mx(out=f_codes[:].bitcast(FP8X4), scales=f_scales[:], in_=fo_woven[:])
+            dst = bank("yo%d" % H, "a%d" % H)
+            product(dst, "wor", f_codes[:].bitcast(FP8X4), f_scales[:])
+            yo.setdefault(H, dst)
+
+        def add_residual(H):
+            y = tile("y%d" % H, [P, PACK, HALF], F32)
+            nc.vector.tensor_tensor(y[:], yo[H][:], res_sb[:, :, halves[H]], ALU.add)
+            nc.sync.dma_start(out=rows4(out_0)[:, :, halves[H]], in_=y[:])
+            return y
+
+        def planes(H, y_woven):
+            nc.vector.quantize_mx(out=y_codes[:, halves[H]].bitcast(FP8X4), scales=y_scales[:, halves[H]], in_=y_woven[:])
+            nc.sync.dma_start(out=words_out[:, halves[H]], in_=y_codes[:, halves[H]].bitcast(I32))
+
+        fo0 = mix(0, lambda: None)
+        fw0 = weave("fw0", fo0, True)
+        quantize_weight("wor", 0, PACK)
+        fo1 = mix(1, lambda: last_layer(0, fw0))
+        fw1 = weave("fw1", fo1, False)
+        last_layer(1, fw1)
+        y0 = add_residual(0)
+        yw0 = weave("yw0", y0, True)
+        y1 = add_residual(1)
+        yw1 = weave("yw1", y1, False)
+        planes(0, yw0)
+        planes(1, yw1)
+        scale_rows = out_2[0].bitcast(I32)
+        for q in range(4):
+            queue = nc.scalar if q % 2 else nc.sync
+            queue.dma_start(out=scale_rows[4 * q:4 * q + 4, :], in_=y_scales[32 * q:32 * q + 4, :].bitcast(I32))

@@ -40,8 +40,8 @@ def tile_attend_tccarrymix_o_pl_kernel(tc, tab_words, tab_scales, dtab_words, dt
         dtab_sc = tile("dtab_sc", [P, T], U8)
         tab_w = tile("tab_w", [P, T], U16)
         dtab_w = tile("dtab_w", [P, T], U16)
-        pieces = {"w1": 1, "w2": 2, "wor": 1}
-        raw = {n: [tile("raw_%s%d" % (n, c), [P, PACK, 512 // k], F32) for c in range(k)] for n, k in (("w1", 1), ("w2", 2), ("wor", 1))}
+        pieces = {"w1": 1, "w2": 2, "wor": 2}
+        raw = {n: [tile("raw_%s%d" % (n, c), [P, PACK, 512 // k], F32) for c in range(k)] for n, k in (("w1", 1), ("w2", 2), ("wor", 2))}
         carry_t = [tile("carry%d" % t, [P, U], F32) for t in range(PACK)]
         res_sb = tile("res_sb", [P, PACK, J], F32)
         bias_sb = tile("bias_sb", [P, PACK], F32)
@@ -66,11 +66,12 @@ def tile_attend_tccarrymix_o_pl_kernel(tc, tab_words, tab_scales, dtab_words, dt
         for c in range(2):
             nc.sync.dma_start(out=raw["w2"][c][:], in_=rows4(w2)[:, :, 256 * c:256 * (c + 1)])
         nc.sync.dma_start(idx2[:], offs2)
-        nc.sync.dma_start(out=bias_sb[:], in_=bias.rearrange("(p t) o -> p (t o)", t=PACK))
-        nc.sync.dma_start(out=rs_sb[:], in_=rs.rearrange("(p t) o -> p (t o)", t=PACK))
+        nc.gpsimd.dma_start(out=bias_sb[:], in_=bias.rearrange("(p t) o -> p (t o)", t=PACK))
+        nc.gpsimd.dma_start(out=rs_sb[:], in_=rs.rearrange("(p t) o -> p (t o)", t=PACK))
         for t in range(PACK):
             nc.sync.dma_start(out=carry_t[t][:], in_=rows4(carry)[:, t, :])
-        nc.sync.dma_start(out=raw["wor"][0][:], in_=rows4(wor))
+        for c in range(2):
+            nc.sync.dma_start(out=raw["wor"][c][:], in_=rows4(wor)[:, :, 256 * c:256 * (c + 1)])
         nc.sync.dma_start(out=res_sb[:], in_=rows4(res))
 
         woven = {n: tile("woven_" + n, [P, PACK * 512], BF16) for n in raw}
@@ -161,9 +162,11 @@ def tile_attend_tccarrymix_o_pl_kernel(tc, tab_words, tab_scales, dtab_words, dt
             for t in range(PACK):
                 nc.scalar.activation(out=s[H][:, t, :], in_=b[H][:, t, :], func=ACT.Tanh, scale=0.5,
                                      bias=half_bias[:, t:t + 1])
-        weave_weight("wor", True, 0, 128)
+        weave_weight("wor", True, 0, 64)
+        weave_weight("wor", True, 64, 128)
 
         pairs = [slice(0, 2), slice(2, 4)]
+        quarters = [slice(0, HALF // 2), slice(HALF // 2, HALF)]
 
         def mix(H, between):
             u2 = tile("u2_%d" % H, [P, PACK, HALF], F32)
@@ -176,24 +179,22 @@ def tile_attend_tccarrymix_o_pl_kernel(tc, tab_words, tab_scales, dtab_words, dt
             for q in pairs:
                 nc.vector.scalar_tensor_tensor(out=u3[:, q, :], in0=s[H][:, q, :], scalar=1.0, in1=u2[:, q, :],
                                                op0=ALU.subtract, op1=ALU.mult)
-            between()
             for t in range(PACK):
                 nc.vector.scalar_tensor_tensor(out=e[:, t, :], in0=u1[:, t, halves[H]], scalar=rs_neg_half[:, t:t + 1],
                                                in1=u3[:, t, :], op0=ALU.mult, op1=ALU.add)
-            for q in pairs:
-                nc.vector.scalar_tensor_tensor(out=fo[:, q, :], in0=s[H][:, q, :], scalar=1.0, in1=e[:, q, :],
+            between()
+            for q in quarters:
+                nc.vector.scalar_tensor_tensor(out=fo[:, :, q], in0=s[H][:, :, q], scalar=1.0, in1=e[:, :, q],
                                                op0=ALU.add, op1=ALU.mult)
             return fo
 
-        def weave(name, src, on_scalar):
-            dst = tile(name, [P, HALF * PACK], BF16)
-            o = dst[:].rearrange("p (c i t) -> p c t i", i=4, t=PACK)
-            i = src[:].rearrange("p t (c i) -> p c t i", i=4)
+        def weave(dst, src, on_scalar, cols):
+            o = dst[:, PACK * cols.start:PACK * cols.stop].rearrange("p (c i t) -> p c t i", i=4, t=PACK)
+            i = src[:, :, cols].rearrange("p t (c i) -> p c t i", i=4)
             if on_scalar:
                 nc.scalar.copy(out=o, in_=i)
             else:
                 nc.vector.tensor_copy(out=o, in_=i)
-            return dst
 
         y_codes = tile("y_codes", [P, J], U32)
         y_scales = tile("y_scales", [P, J], U8)
@@ -209,9 +210,10 @@ def tile_attend_tccarrymix_o_pl_kernel(tc, tab_words, tab_scales, dtab_words, dt
             product(dst, "wor", f_codes[:].bitcast(FP8X4), f_scales[:])
             yo.setdefault(H, dst)
 
-        def add_residual(H):
+        def add_residual(H, parts):
             y = tile("y%d" % H, [P, PACK, HALF], F32)
-            nc.vector.tensor_tensor(y[:], yo[H][:], res_sb[:, :, halves[H]], ALU.add)
+            for q in parts:
+                nc.vector.tensor_tensor(y[:, :, q], yo[H][:, :, q], res_sb[:, :, halves[H]][:, :, q], ALU.add)
             nc.sync.dma_start(out=rows4(out_0)[:, :, halves[H]], in_=y[:])
             return y
 
@@ -219,19 +221,28 @@ def tile_attend_tccarrymix_o_pl_kernel(tc, tab_words, tab_scales, dtab_words, dt
             nc.vector.quantize_mx(out=y_codes[:, halves[H]].bitcast(FP8X4), scales=y_scales[:, halves[H]], in_=y_woven[:])
             nc.sync.dma_start(out=words_out[:, halves[H]], in_=y_codes[:, halves[H]].bitcast(I32))
 
+        whole = slice(0, HALF)
+        fw = [tile("fw%d" % H, [P, HALF * PACK], BF16) for H in range(2)]
+        yw = [tile("yw%d" % H, [P, HALF * PACK], BF16) for H in range(2)]
         fo0 = mix(0, lambda: None)
-        fw0 = weave("fw0", fo0, True)
-        quantize_weight("wor", 0, PACK)
-        fo1 = mix(1, lambda: last_layer(0, fw0))
-        fw1 = weave("fw1", fo1, False)
-        last_layer(1, fw1)
-        y0 = add_residual(0)
-        yw0 = weave("yw0", y0, True)
-        y1 = add_residual(1)
-        yw1 = weave("yw1", y1, False)
-        planes(0, yw0)
-        planes(1, yw1)
+        weave(fw[0], fo0, True, whole)
+
+        def first_half_on():
+            quantize_weight("wor", 0, PACK)
+            last_layer(0, fw[0])
+
+        fo1 = mix(1, first_half_on)
+        weave(fw[1], fo1, True, quarters[0])
+        weave(fw[1], fo1, False, quarters[1])
+        last_layer(1, fw[1])
+        y0 = add_residual(0, [whole])
+        weave(yw[0], y0, True, whole)
+        y1 = add_residual(1, quarters)
+        weave(yw[1], y1, True, quarters[0])
+        planes(0, yw[0])
+        weave(yw[1], y1, False, quarters[1])
+        planes(1, yw[1])
         scale_rows = out_2[0].bitcast(I32)
         for q in range(4):
-            queue = nc.scalar if q % 2 else nc.sync
+            queue = nc.scalar if q < 3 else nc.sync
             queue.dma_start(out=scale_rows[4 * q:4 * q + 4, :], in_=y_scales[32 * q:32 * q + 4, :].bitcast(I32))

@@ -2,7 +2,7 @@ from contextlib import ExitStack
 
 import concourse.mybir as mybir
 
-K, R, F, T, J, U = 512, 512, 512, 2048, 256, 512
+R, T, J, U = 512, 2048, 256, 512
 FLOPS = 671088640
 
 F32 = mybir.dt.float32
@@ -17,8 +17,10 @@ ALU = mybir.AluOpType
 ACT = mybir.ActivationFunctionType
 
 P = 128
-PACK = 4
+SLOTS = 4
 HALF = J // 2
+QUARTER = J // 4
+M_HALF = P // 2
 
 
 def tile_attend_tccarrymix_o_pl_kernel(tc, tab_words, tab_scales, dtab_words, dtab_scales, w1, w2, bias, carry, rs,
@@ -31,8 +33,8 @@ def tile_attend_tccarrymix_o_pl_kernel(tc, tab_words, tab_scales, dtab_words, dt
         def tile(name, shape, dtype):
             return sb.tile(shape, dtype, name=name, align_bytes=64)
 
-        def bank(name, tag):
-            return psum.tile([P, PACK, HALF], F32, name=name, tag=tag)
+        def by_slot(dram):
+            return dram.rearrange("(p t) c -> p t c", t=SLOTS)
 
         idx = sb.tile([P, J // 16], U16, name="idx")
         idx2 = sb.tile([P, J // 16], U16, name="idx2")
@@ -40,209 +42,208 @@ def tile_attend_tccarrymix_o_pl_kernel(tc, tab_words, tab_scales, dtab_words, dt
         dtab_sc = tile("dtab_sc", [P, T], U8)
         tab_w = tile("tab_w", [P, T], U16)
         dtab_w = tile("dtab_w", [P, T], U16)
-        pieces = {"w1": 1, "w2": 2, "wor": 2}
-        raw = {n: [tile("raw_%s%d" % (n, c), [P, PACK, 512 // k], F32) for c in range(k)] for n, k in (("w1", 1), ("w2", 2), ("wor", 2))}
-        carry_t = [tile("carry%d" % t, [P, U], F32) for t in range(PACK)]
-        res_sb = tile("res_sb", [P, PACK, J], F32)
-        bias_sb = tile("bias_sb", [P, PACK], F32)
-        rs_sb = tile("rs_sb", [P, PACK], F32)
+        w1_raw = tile("w1_raw", [P, SLOTS, R], F32)
+        w2_raw = tile("w2_raw", [P, SLOTS, R], F32)
+        wor_raw = [tile("wor_raw%d" % c, [P, SLOTS, R // 2], F32) for c in range(2)]
+        carry_sb = [tile("carry%d" % t, [P, U], F32) for t in range(SLOTS)]
+        res_sb = tile("res_sb", [P, SLOTS, J], F32)
+        bias_sb = tile("bias_sb", [P, SLOTS], F32)
+        rs_sb = tile("rs_sb", [P, SLOTS], F32)
 
-        def load_scales(queue, dst, src):
-            rows = src[0].bitcast(I32).rearrange("(q i) c -> i q c", i=4)
+        def load_scale_rows(window, dram):
+            rows = dram[0].bitcast(I32).rearrange("(q i) c -> i q c", i=4)
             for i in range(4):
-                queue.dma_start(out=dst[i:P:32, :].bitcast(I32), in_=rows[i])
-
-        def rows4(src):
-            return src.rearrange("(p t) c -> p t c", t=PACK)
+                nc.sync.dma_start(out=window[i:P:32, :].bitcast(I32), in_=rows[i])
 
         nc.vector.memset(tab_sc[:].bitcast(I32), 0)
         nc.vector.memset(dtab_sc[:].bitcast(I32), 0)
+        nc.sync.dma_start(out=w1_raw[:], in_=by_slot(w1))
         nc.sync.dma_start(idx[:], offs)
-        nc.sync.dma_start(out=raw["w1"][0][:], in_=rows4(w1))
-        load_scales(nc.sync, tab_sc, tab_scales)
+        load_scale_rows(tab_sc, tab_scales)
         nc.sync.dma_start(out=tab_w[:].bitcast(I32), in_=tab_words[0].bitcast(I32))
         nc.sync.dma_start(out=dtab_w[:].bitcast(I32), in_=dtab_words[0].bitcast(I32))
-        load_scales(nc.sync, dtab_sc, dtab_scales)
-        for c in range(2):
-            nc.sync.dma_start(out=raw["w2"][c][:], in_=rows4(w2)[:, :, 256 * c:256 * (c + 1)])
+        load_scale_rows(dtab_sc, dtab_scales)
+        nc.sync.dma_start(out=w2_raw[:], in_=by_slot(w2))
         nc.sync.dma_start(idx2[:], offs2)
-        nc.gpsimd.dma_start(out=bias_sb[:], in_=bias.rearrange("(p t) o -> p (t o)", t=PACK))
-        nc.gpsimd.dma_start(out=rs_sb[:], in_=rs.rearrange("(p t) o -> p (t o)", t=PACK))
-        for t in range(PACK):
-            nc.sync.dma_start(out=carry_t[t][:], in_=rows4(carry)[:, t, :])
+        nc.gpsimd.dma_start(out=bias_sb[:], in_=bias.rearrange("(p t) o -> p (t o)", t=SLOTS))
+        nc.gpsimd.dma_start(out=rs_sb[:], in_=rs.rearrange("(p t) o -> p (t o)", t=SLOTS))
+        for t in range(SLOTS):
+            nc.sync.dma_start(out=carry_sb[t][:], in_=by_slot(carry)[:, t, :])
         for c in range(2):
-            nc.sync.dma_start(out=raw["wor"][c][:], in_=rows4(wor)[:, :, 256 * c:256 * (c + 1)])
-        nc.sync.dma_start(out=res_sb[:], in_=rows4(res))
+            nc.sync.dma_start(out=wor_raw[c][:], in_=by_slot(wor)[:, :, c * R // 2:(c + 1) * R // 2])
+        nc.sync.dma_start(out=res_sb[:], in_=by_slot(res))
 
-        woven = {n: tile("woven_" + n, [P, PACK * 512], BF16) for n in raw}
-        codes = {n: tile("codes_" + n, [P, 512], U32) for n in raw}
-        scales = {n: tile("scales_" + n, [P, 512], U8) for n in raw}
+        names = ("w1", "w2", "wor")
+        grouped = {n: tile("grouped_" + n, [P, SLOTS * R], BF16) for n in names}
+        codes = {n: tile("codes_" + n, [P, R], U32) for n in names}
+        scales = {n: tile("scales_" + n, [P, R], U8) for n in names}
 
-        def weave_weight(n, on_scalar, m0, m1):
-            dst = woven[n][:].rearrange("p (t m j) -> p m j t", t=PACK, j=PACK)[:, m0:m1]
-            per = P // pieces[n]
-            c = m0 // per
-            src = raw[n][c][:].rearrange("p j (m t) -> p m j t", t=PACK)[:, m0 - c * per:m1 - c * per]
-            if on_scalar:
-                nc.scalar.activation(out=dst, in_=src, func=ACT.Copy)
-            else:
-                nc.vector.tensor_copy(out=dst, in_=src)
+        def scalar_cast(out, in_):
+            nc.scalar.activation(out=out, in_=in_, func=ACT.Copy)
 
-        def quantize_weight(n, t0, t1):
-            nc.vector.quantize_mx(out=codes[n][:, P * t0:P * t1].bitcast(FP8X4), scales=scales[n][:, P * t0:P * t1],
-                                  in_=woven[n][:, 512 * t0:512 * t1])
+        def group_weight(copy, n, half, raw):
+            dst = grouped[n][:].rearrange("p (t m j) -> p m t j", t=SLOTS, j=SLOTS)
+            copy(dst[:, M_HALF * half:M_HALF * (half + 1)], raw.rearrange("p j (m t) -> p m t j", t=SLOTS))
+
+        def quantize_weight(n, slots):
+            cols = slice(P * slots.start, P * slots.stop)
+            nc.vector.quantize_mx(out=codes[n][:, cols].bitcast(FP8X4), scales=scales[n][:, cols],
+                                  in_=grouped[n][:, R * slots.start:R * slots.stop])
 
         def gather(name, window, dtype):
-            got = tile(name, [P, J], dtype)
-            nc.vector.tensor_copy(out=got[:], in_=window[:].indirect(idx[:]))
-            return got
+            listed = tile(name, [P, J], dtype)
+            nc.vector.tensor_copy(out=listed[:], in_=window[:].indirect(idx[:]))
+            return listed
 
-        def product(dst, n, rhs, rhs_scale):
-            for t in range(PACK):
+        def product(bank, n, slots, moving, moving_scales):
+            for t in range(slots.start, slots.stop):
                 cols = slice(P * t, P * (t + 1))
-                nc.tensor.matmul_mx(out=dst[:, t, :], lhsT=codes[n][:, cols].bitcast(FP8X4), lhsT_scale=scales[n][:, cols],
-                                    rhs=rhs, rhs_scale=rhs_scale, start=True, stop=True)
-
-        halves = [slice(HALF * H, HALF * (H + 1)) for H in range(2)]
-
-        def first_layer(name, n, words, sc, H):
-            dst = bank("%s%d" % (name, H), "%s%d" % (name, H))
-            product(dst, n, words[:, halves[H]].bitcast(FP4X4), sc[:, halves[H]])
-            return dst
-
-        weave_weight("w1", True, 0, 64)
-        weave_weight("w1", False, 64, 128)
-        g_tab_sc = gather("g_tab_sc", tab_sc, U8)
-        for t in range(PACK):
-            quantize_weight("w1", t, t + 1)
-        g_tab_w = gather("g_tab_w", tab_w, U16)
-        a = [first_layer("a", "w1", g_tab_w, g_tab_sc, H) for H in range(2)]
-        g_dtab_w = gather("g_dtab_w", dtab_w, U16)
-        g_dtab_sc = gather("g_dtab_sc", dtab_sc, U8)
-        ta = [first_layer("ta", "w1", g_dtab_w, g_dtab_sc, H) for H in range(2)]
-
-        half_bias = tile("half_bias", [P, PACK], F32)
-        rs_quarter = tile("rs_quarter", [P, PACK], F32)
-        rs_neg_half = tile("rs_neg_half", [P, PACK], F32)
-        nc.gpsimd.tensor_scalar(out=half_bias[:], in0=bias_sb[:], scalar1=0.5, scalar2=0.0, op0=ALU.mult, op1=ALU.add)
-        nc.gpsimd.tensor_scalar(out=rs_quarter[:], in0=rs_sb[:], scalar1=0.25, scalar2=0.0, op0=ALU.mult, op1=ALU.add)
-        nc.gpsimd.tensor_scalar(out=rs_neg_half[:], in0=rs_sb[:], scalar1=-0.5, scalar2=0.0, op0=ALU.mult, op1=ALU.add)
-
-        h = tile("h", [P, PACK, J], F32)
-        hsq = tile("hsq", [P, PACK, J], F32)
-        u1 = tile("u1", [P, PACK, J], F32)
-        d = tile("d", [P, PACK, J], F32)
-        for H in range(2):
-            nc.scalar.activation(out=h[:, :, halves[H]], in_=a[H][:], func=ACT.Tanh)
-        for H in range(2):
-            nc.scalar.activation(out=hsq[:, :, halves[H]], in_=h[:, :, halves[H]], func=ACT.Square)
-
-        def th1(H):
-            nc.vector.scalar_tensor_tensor(out=u1[:, :, halves[H]], in0=hsq[:, :, halves[H]], scalar=1.0, in1=ta[H][:],
-                                           op0=ALU.subtract, op1=ALU.mult)
-
-        def carry_minus_h(t):
-            nc.vector.tensor_tensor(d[:, t, :], carry_t[t][:].indirect(idx2[:]), h[:, t, :], ALU.subtract)
-
-        weave_weight("w2", False, 0, 64)
-        weave_weight("w2", True, 64, 128)
-        th1(0)
-        th1(1)
-        carry_minus_h(0)
-        for t in range(PACK):
-            quantize_weight("w2", t, t + 1)
-        b, tb = [], []
-        for H in range(2):
-            b.append(first_layer("b", "w2", g_tab_w, g_tab_sc, H))
-            tb.append(first_layer("tb", "w2", g_dtab_w, g_dtab_sc, H))
-        for t in range(1, PACK):
-            carry_minus_h(t)
-        s = [tile("s%d" % H, [P, PACK, HALF], F32) for H in range(2)]
-        for H in range(2):
-            for t in range(PACK):
-                nc.scalar.activation(out=s[H][:, t, :], in_=b[H][:, t, :], func=ACT.Tanh, scale=0.5,
-                                     bias=half_bias[:, t:t + 1])
-        weave_weight("wor", True, 0, 64)
-        weave_weight("wor", True, 64, 128)
+                nc.tensor.matmul_mx(out=bank[:, t - slots.start, :], lhsT=codes[n][:, cols].bitcast(FP8X4),
+                                    lhsT_scale=scales[n][:, cols], rhs=moving, rhs_scale=moving_scales,
+                                    start=True, stop=True)
 
         pairs = [slice(0, 2), slice(2, 4)]
-        quarters = [slice(0, HALF // 2), slice(HALF // 2, HALF)]
+        all_slots = slice(0, SLOTS)
 
-        def mix(H, between):
-            u2 = tile("u2_%d" % H, [P, PACK, HALF], F32)
-            u3 = tile("u3_%d" % H, [P, PACK, HALF], F32)
-            e = tile("e_%d" % H, [P, PACK, HALF], F32)
-            fo = tile("fo_%d" % H, [P, PACK, HALF], BF16)
-            for t in range(PACK):
-                nc.vector.scalar_tensor_tensor(out=u2[:, t, :], in0=tb[H][:, t, :], scalar=rs_quarter[:, t:t + 1],
-                                               in1=d[:, t, halves[H]], op0=ALU.mult, op1=ALU.mult)
-            for q in pairs:
-                nc.vector.scalar_tensor_tensor(out=u3[:, q, :], in0=s[H][:, q, :], scalar=1.0, in1=u2[:, q, :],
-                                               op0=ALU.subtract, op1=ALU.mult)
-            for t in range(PACK):
-                nc.vector.scalar_tensor_tensor(out=e[:, t, :], in0=u1[:, t, halves[H]], scalar=rs_neg_half[:, t:t + 1],
-                                               in1=u3[:, t, :], op0=ALU.mult, op1=ALU.add)
-            between()
-            for q in quarters:
-                nc.vector.scalar_tensor_tensor(out=fo[:, :, q], in0=s[H][:, :, q], scalar=1.0, in1=e[:, :, q],
-                                               op0=ALU.add, op1=ALU.mult)
-            return fo
+        def first_layer(name, n, words, word_scales, q):
+            bank = psum.tile([P, 2, J], F32, name="%s%d" % (name, q), tag="%s%d" % (name, q))
+            product(bank, n, pairs[q], words[:].bitcast(FP4X4), word_scales[:])
+            return bank
 
-        def weave(dst, src, on_scalar, cols):
-            o = dst[:, PACK * cols.start:PACK * cols.stop].rearrange("p (c i t) -> p c t i", i=4, t=PACK)
-            i = src[:, :, cols].rearrange("p t (c i) -> p c t i", i=4)
-            if on_scalar:
-                nc.scalar.copy(out=o, in_=i)
-            else:
-                nc.vector.tensor_copy(out=o, in_=i)
+        group_weight(scalar_cast, "w1", 0, w1_raw[:, :, :R // 2])
+        group_weight(nc.vector.tensor_copy, "w1", 1, w1_raw[:, :, R // 2:])
+        tab_sc_listed = gather("tab_sc_listed", tab_sc, U8)
+        quantize_weight("w1", pairs[0])
+        tab_listed = gather("tab_listed", tab_w, U16)
+        quantize_weight("w1", pairs[1])
+        a = [first_layer("a", "w1", tab_listed, tab_sc_listed, q) for q in range(2)]
+        dtab_listed = gather("dtab_listed", dtab_w, U16)
+        dtab_sc_listed = gather("dtab_sc_listed", dtab_sc, U8)
+        ta = [first_layer("ta", "w1", dtab_listed, dtab_sc_listed, q) for q in range(2)]
 
+        def scaled(name, vector, factor):
+            out = tile(name, [P, SLOTS], F32)
+            nc.gpsimd.tensor_scalar(out=out[:], in0=vector[:], scalar1=factor, scalar2=0.0, op0=ALU.mult, op1=ALU.add)
+            return out
+
+        half_bias = scaled("half_bias", bias_sb, 0.5)
+        quarter_rs = scaled("quarter_rs", rs_sb, 0.25)
+        minus_half_rs = scaled("minus_half_rs", rs_sb, -0.5)
+
+        def wide(name):
+            return tile(name, [P, SLOTS, J], F32)
+
+        h1, h1_sq, minus_th1, gap = wide("h1"), wide("h1_sq"), wide("minus_th1"), wide("gap")
+        s, tb_gap, gate_term, inner = wide("s"), wide("tb_gap"), wide("gate_term"), wide("inner")
+        fo1 = tile("fo1", [P, SLOTS, J], BF16)
+        for q in range(2):
+            nc.scalar.activation(out=h1[:, pairs[q], :], in_=a[q][:], func=ACT.Tanh)
+            nc.scalar.activation(out=h1_sq[:, pairs[q], :], in_=h1[:, pairs[q], :], func=ACT.Square)
+
+        def carry_minus_h1(t):
+            nc.vector.tensor_tensor(gap[:, t, :], carry_sb[t][:].indirect(idx2[:]), h1[:, t, :], ALU.subtract)
+
+        group_weight(nc.vector.tensor_copy, "w2", 0, w2_raw[:, :, :R // 2])
+        group_weight(scalar_cast, "w2", 1, w2_raw[:, :, R // 2:])
+        for q in range(2):
+            nc.vector.scalar_tensor_tensor(out=minus_th1[:, pairs[q], :], in0=h1_sq[:, pairs[q], :], scalar=1.0,
+                                           in1=ta[q][:], op0=ALU.subtract, op1=ALU.mult)
+        carry_minus_h1(0)
+        for q in range(2):
+            quantize_weight("w2", pairs[q])
+        b, tb = [], []
+        for q in range(2):
+            b.append(first_layer("b", "w2", tab_listed, tab_sc_listed, q))
+            tb.append(first_layer("tb", "w2", dtab_listed, dtab_sc_listed, q))
+        for t in range(1, SLOTS):
+            carry_minus_h1(t)
+        for t in range(SLOTS):
+            nc.scalar.activation(out=s[:, t, :], in_=b[t // 2][:, t % 2, :], func=ACT.Tanh, scale=0.5,
+                                 bias=half_bias[:, t:t + 1])
+        for c in range(2):
+            group_weight(scalar_cast, "wor", c, wor_raw[c][:])
+
+        for t in range(SLOTS):
+            nc.vector.scalar_tensor_tensor(out=tb_gap[:, t, :], in0=tb[t // 2][:, t % 2, :],
+                                           scalar=quarter_rs[:, t:t + 1], in1=gap[:, t, :], op0=ALU.mult, op1=ALU.mult)
+        for q in range(2):
+            nc.vector.scalar_tensor_tensor(out=gate_term[:, pairs[q], :], in0=s[:, pairs[q], :], scalar=1.0,
+                                           in1=tb_gap[:, pairs[q], :], op0=ALU.subtract, op1=ALU.mult)
+        for t in range(SLOTS):
+            nc.vector.scalar_tensor_tensor(out=inner[:, t, :], in0=minus_th1[:, t, :],
+                                           scalar=minus_half_rs[:, t:t + 1], in1=gate_term[:, t, :],
+                                           op0=ALU.mult, op1=ALU.add)
+
+        def finish_fo1(cols):
+            nc.vector.scalar_tensor_tensor(out=fo1[:, :, cols], in0=s[:, :, cols], scalar=1.0, in1=inner[:, :, cols],
+                                           op0=ALU.add, op1=ALU.mult)
+
+        halves = [slice(0, HALF), slice(HALF, J)]
+        third_quarter, last_quarter = slice(HALF, HALF + QUARTER), slice(HALF + QUARTER, J)
+        fo1_grouped = [tile("fo1_grouped%d" % k, [P, SLOTS * HALF], BF16) for k in range(2)]
+        y_grouped = [tile("y_grouped%d" % k, [P, SLOTS * HALF], BF16) for k in range(2)]
+        y = [tile("y%d" % k, [P, SLOTS, HALF], F32) for k in range(2)]
         y_codes = tile("y_codes", [P, J], U32)
         y_scales = tile("y_scales", [P, J], U8)
         words_out = out_1[0].rearrange("p c r -> p (c r)").bitcast(I32)
 
-        yo = {}
+        def in_half(cols):
+            k = cols.start // HALF
+            return k, slice(cols.start - k * HALF, cols.stop - k * HALF)
 
-        def last_layer(H, fo_woven):
-            f_codes = tile("f_codes%d" % H, [P, HALF], U32)
-            f_scales = tile("f_scales%d" % H, [P, HALF], U8)
-            nc.vector.quantize_mx(out=f_codes[:].bitcast(FP8X4), scales=f_scales[:], in_=fo_woven[:])
-            dst = bank("yo%d" % H, "a%d" % H)
-            product(dst, "wor", f_codes[:].bitcast(FP8X4), f_scales[:])
-            yo.setdefault(H, dst)
+        def group_slots(copy, dst, cols, src):
+            k, part = in_half(cols)
+            out = dst[k][:, SLOTS * part.start:SLOTS * part.stop].rearrange("p (c i t) -> p c t i", i=4, t=SLOTS)
+            copy(out, src.rearrange("p t (c i) -> p c t i", i=4))
 
-        def add_residual(H, parts):
-            y = tile("y%d" % H, [P, PACK, HALF], F32)
-            for q in parts:
-                nc.vector.tensor_tensor(y[:, :, q], yo[H][:, :, q], res_sb[:, :, halves[H]][:, :, q], ALU.add)
-            nc.sync.dma_start(out=rows4(out_0)[:, :, halves[H]], in_=y[:])
-            return y
+        def group_fo1(copy, cols):
+            group_slots(copy, fo1_grouped, cols, fo1[:, :, cols])
 
-        def planes(H, y_woven):
-            nc.vector.quantize_mx(out=y_codes[:, halves[H]].bitcast(FP8X4), scales=y_scales[:, halves[H]], in_=y_woven[:])
-            nc.sync.dma_start(out=words_out[:, halves[H]], in_=y_codes[:, halves[H]].bitcast(I32))
+        def group_y(copy, cols):
+            k, part = in_half(cols)
+            group_slots(copy, y_grouped, cols, y[k][:, :, part])
 
-        whole = slice(0, HALF)
-        fw = [tile("fw%d" % H, [P, HALF * PACK], BF16) for H in range(2)]
-        yw = [tile("yw%d" % H, [P, HALF * PACK], BF16) for H in range(2)]
-        fo0 = mix(0, lambda: None)
-        weave(fw[0], fo0, True, whole)
+        def last_layer(k):
+            fo1_codes = tile("fo1_codes%d" % k, [P, HALF], U32)
+            fo1_scales = tile("fo1_scales%d" % k, [P, HALF], U8)
+            nc.vector.quantize_mx(out=fo1_codes[:].bitcast(FP8X4), scales=fo1_scales[:], in_=fo1_grouped[k][:])
+            bank = psum.tile([P, SLOTS, HALF], F32, name="yo%d" % k, tag="a%d" % k)
+            product(bank, "wor", all_slots, fo1_codes[:].bitcast(FP8X4), fo1_scales[:])
+            return bank
 
-        def first_half_on():
-            quantize_weight("wor", 0, PACK)
-            last_layer(0, fw[0])
+        def add_residual(yo, cols):
+            k, part = in_half(cols)
+            nc.vector.tensor_tensor(y[k][:, :, part], yo[:, :, part], res_sb[:, :, cols], ALU.add)
 
-        fo1 = mix(1, first_half_on)
-        weave(fw[1], fo1, True, quarters[0])
-        weave(fw[1], fo1, False, quarters[1])
-        last_layer(1, fw[1])
-        y0 = add_residual(0, [whole])
-        weave(yw[0], y0, True, whole)
-        y1 = add_residual(1, quarters)
-        weave(yw[1], y1, True, quarters[0])
-        planes(0, yw[0])
-        weave(yw[1], y1, False, quarters[1])
-        planes(1, yw[1])
+        def store_y(k):
+            nc.sync.dma_start(out=by_slot(out_0)[:, :, halves[k]], in_=y[k][:])
+
+        def planes(k):
+            cols = halves[k]
+            nc.vector.quantize_mx(out=y_codes[:, cols].bitcast(FP8X4), scales=y_scales[:, cols], in_=y_grouped[k][:])
+            nc.sync.dma_start(out=words_out[:, cols], in_=y_codes[:, cols].bitcast(I32))
+
+        finish_fo1(halves[0])
+        group_fo1(nc.scalar.copy, halves[0])
+        quantize_weight("wor", all_slots)
+        finish_fo1(third_quarter)
+        group_fo1(nc.scalar.copy, third_quarter)
+        finish_fo1(last_quarter)
+        yo_first = last_layer(0)
+        group_fo1(nc.vector.tensor_copy, last_quarter)
+        yo_second = last_layer(1)
+        add_residual(yo_first, halves[0])
+        store_y(0)
+        group_y(nc.scalar.copy, halves[0])
+        add_residual(yo_second, third_quarter)
+        add_residual(yo_second, last_quarter)
+        store_y(1)
+        group_y(nc.scalar.copy, third_quarter)
+        planes(0)
+        group_y(nc.vector.tensor_copy, last_quarter)
+        planes(1)
+
         scale_rows = out_2[0].bitcast(I32)
-        for q in range(4):
-            queue = nc.scalar if q < 3 else nc.sync
-            queue.dma_start(out=scale_rows[4 * q:4 * q + 4, :], in_=y_scales[32 * q:32 * q + 4, :].bitcast(I32))
+        for quadrant, queue in enumerate((nc.scalar, nc.scalar, nc.scalar, nc.sync)):
+            queue.dma_start(out=scale_rows[4 * quadrant:4 * quadrant + 4, :],
+                            in_=y_scales[32 * quadrant:32 * quadrant + 4, :].bitcast(I32))

from contextlib import ExitStack

import concourse.mybir as mybir

R, T, J, U = 512, 2048, 256, 512
FLOPS = 671088640

F32 = mybir.dt.float32
BF16 = mybir.dt.bfloat16
I32 = mybir.dt.int32
U32 = mybir.dt.uint32
U16 = mybir.dt.uint16
U8 = mybir.dt.uint8
FP8X4 = mybir.dt.float8_e4m3fn_x4
FP4X4 = mybir.dt.float4_e2m1fn_x4
ALU = mybir.AluOpType
ACT = mybir.ActivationFunctionType

P = 128
SLOTS = 4
HALF = J // 2
QUARTER = J // 4
M_HALF = P // 2


def tile_attend_tccarrymix_o_pl_kernel(tc, tab_words, tab_scales, dtab_words, dtab_scales, w1, w2, bias, carry, rs,
                                        wor, res, offs, offs2, out_0, out_1, out_2):
    nc = tc.nc
    with ExitStack() as ctx:
        sb = ctx.enter_context(tc.tile_pool(name="sb", bufs=1))
        psum = ctx.enter_context(tc.psum_pool(name="psum", bufs=1))

        def tile(name, shape, dtype):
            return sb.tile(shape, dtype, name=name, align_bytes=64)

        def by_slot(dram):
            return dram.rearrange("(p t) c -> p t c", t=SLOTS)

        idx = sb.tile([P, J // 16], U16, name="idx")
        idx2 = sb.tile([P, J // 16], U16, name="idx2")
        tab_sc = tile("tab_sc", [P, T], U8)
        dtab_sc = tile("dtab_sc", [P, T], U8)
        tab_w = tile("tab_w", [P, T], U16)
        dtab_w = tile("dtab_w", [P, T], U16)
        w1_raw = tile("w1_raw", [P, SLOTS, R], F32)
        w2_raw = tile("w2_raw", [P, SLOTS, R], F32)
        wor_raw = [tile("wor_raw%d" % c, [P, SLOTS, R // 2], F32) for c in range(2)]
        carry_sb = [tile("carry%d" % t, [P, U], F32) for t in range(SLOTS)]
        res_sb = tile("res_sb", [P, SLOTS, J], F32)
        bias_sb = tile("bias_sb", [P, SLOTS], F32)
        rs_sb = tile("rs_sb", [P, SLOTS], F32)

        def load_scale_rows(window, dram):
            rows = dram[0].bitcast(I32).rearrange("(q i) c -> i q c", i=4)
            for i in range(4):
                nc.sync.dma_start(out=window[i:P:32, :].bitcast(I32), in_=rows[i])

        nc.vector.memset(tab_sc[:].bitcast(I32), 0)
        nc.vector.memset(dtab_sc[:].bitcast(I32), 0)
        nc.sync.dma_start(out=w1_raw[:], in_=by_slot(w1))
        nc.sync.dma_start(idx[:], offs)
        load_scale_rows(tab_sc, tab_scales)
        nc.sync.dma_start(out=tab_w[:].bitcast(I32), in_=tab_words[0].bitcast(I32))
        nc.sync.dma_start(out=dtab_w[:].bitcast(I32), in_=dtab_words[0].bitcast(I32))
        load_scale_rows(dtab_sc, dtab_scales)
        nc.sync.dma_start(out=w2_raw[:], in_=by_slot(w2))
        nc.sync.dma_start(idx2[:], offs2)
        nc.gpsimd.dma_start(out=bias_sb[:], in_=bias.rearrange("(p t) o -> p (t o)", t=SLOTS))
        nc.gpsimd.dma_start(out=rs_sb[:], in_=rs.rearrange("(p t) o -> p (t o)", t=SLOTS))
        for t in range(SLOTS):
            nc.sync.dma_start(out=carry_sb[t][:], in_=by_slot(carry)[:, t, :])
        for c in range(2):
            nc.sync.dma_start(out=wor_raw[c][:], in_=by_slot(wor)[:, :, c * R // 2:(c + 1) * R // 2])
        nc.sync.dma_start(out=res_sb[:], in_=by_slot(res))

        names = ("w1", "w2", "wor")
        grouped = {n: tile("grouped_" + n, [P, SLOTS * R], BF16) for n in names}
        codes = {n: tile("codes_" + n, [P, R], U32) for n in names}
        scales = {n: tile("scales_" + n, [P, R], U8) for n in names}

        def scalar_cast(out, in_):
            nc.scalar.activation(out=out, in_=in_, func=ACT.Copy)

        def group_weight(copy, n, half, raw):
            dst = grouped[n][:].rearrange("p (t m j) -> p m t j", t=SLOTS, j=SLOTS)
            copy(dst[:, M_HALF * half:M_HALF * (half + 1)], raw.rearrange("p j (m t) -> p m t j", t=SLOTS))

        def quantize_weight(n, slots):
            cols = slice(P * slots.start, P * slots.stop)
            nc.vector.quantize_mx(out=codes[n][:, cols].bitcast(FP8X4), scales=scales[n][:, cols],
                                  in_=grouped[n][:, R * slots.start:R * slots.stop])

        def gather(name, window, dtype):
            listed = tile(name, [P, J], dtype)
            nc.vector.tensor_copy(out=listed[:], in_=window[:].indirect(idx[:]))
            return listed

        def product(bank, n, slots, moving, moving_scales):
            for t in range(slots.start, slots.stop):
                cols = slice(P * t, P * (t + 1))
                nc.tensor.matmul_mx(out=bank[:, t - slots.start, :], lhsT=codes[n][:, cols].bitcast(FP8X4),
                                    lhsT_scale=scales[n][:, cols], rhs=moving, rhs_scale=moving_scales,
                                    start=True, stop=True)

        pairs = [slice(0, 2), slice(2, 4)]
        all_slots = slice(0, SLOTS)

        def first_layer(name, n, words, word_scales, q):
            bank = psum.tile([P, 2, J], F32, name="%s%d" % (name, q), tag="%s%d" % (name, q))
            product(bank, n, pairs[q], words[:].bitcast(FP4X4), word_scales[:])
            return bank

        group_weight(scalar_cast, "w1", 0, w1_raw[:, :, :R // 2])
        group_weight(nc.vector.tensor_copy, "w1", 1, w1_raw[:, :, R // 2:])
        tab_sc_listed = gather("tab_sc_listed", tab_sc, U8)
        quantize_weight("w1", pairs[0])
        tab_listed = gather("tab_listed", tab_w, U16)
        quantize_weight("w1", pairs[1])
        a = [first_layer("a", "w1", tab_listed, tab_sc_listed, q) for q in range(2)]
        dtab_listed = gather("dtab_listed", dtab_w, U16)
        dtab_sc_listed = gather("dtab_sc_listed", dtab_sc, U8)
        ta = [first_layer("ta", "w1", dtab_listed, dtab_sc_listed, q) for q in range(2)]

        def scaled(name, vector, factor):
            out = tile(name, [P, SLOTS], F32)
            nc.gpsimd.tensor_scalar(out=out[:], in0=vector[:], scalar1=factor, scalar2=0.0, op0=ALU.mult, op1=ALU.add)
            return out

        half_bias = scaled("half_bias", bias_sb, 0.5)
        quarter_rs = scaled("quarter_rs", rs_sb, 0.25)
        minus_half_rs = scaled("minus_half_rs", rs_sb, -0.5)

        def wide(name):
            return tile(name, [P, SLOTS, J], F32)

        h1, h1_sq, minus_th1, gap = wide("h1"), wide("h1_sq"), wide("minus_th1"), wide("gap")
        s, tb_gap, gate_term, inner = wide("s"), wide("tb_gap"), wide("gate_term"), wide("inner")
        fo1 = tile("fo1", [P, SLOTS, J], BF16)
        for q in range(2):
            nc.scalar.activation(out=h1[:, pairs[q], :], in_=a[q][:], func=ACT.Tanh)
            nc.scalar.activation(out=h1_sq[:, pairs[q], :], in_=h1[:, pairs[q], :], func=ACT.Square)

        def carry_minus_h1(t):
            nc.vector.tensor_tensor(gap[:, t, :], carry_sb[t][:].indirect(idx2[:]), h1[:, t, :], ALU.subtract)

        group_weight(nc.vector.tensor_copy, "w2", 0, w2_raw[:, :, :R // 2])
        group_weight(scalar_cast, "w2", 1, w2_raw[:, :, R // 2:])
        for q in range(2):
            nc.vector.scalar_tensor_tensor(out=minus_th1[:, pairs[q], :], in0=h1_sq[:, pairs[q], :], scalar=1.0,
                                           in1=ta[q][:], op0=ALU.subtract, op1=ALU.mult)
        carry_minus_h1(0)
        for q in range(2):
            quantize_weight("w2", pairs[q])
        b, tb = [], []
        for q in range(2):
            b.append(first_layer("b", "w2", tab_listed, tab_sc_listed, q))
            tb.append(first_layer("tb", "w2", dtab_listed, dtab_sc_listed, q))
        for t in range(1, SLOTS):
            carry_minus_h1(t)
        for t in range(SLOTS):
            nc.scalar.activation(out=s[:, t, :], in_=b[t // 2][:, t % 2, :], func=ACT.Tanh, scale=0.5,
                                 bias=half_bias[:, t:t + 1])
        for c in range(2):
            group_weight(scalar_cast, "wor", c, wor_raw[c][:])

        for t in range(SLOTS):
            nc.vector.scalar_tensor_tensor(out=tb_gap[:, t, :], in0=tb[t // 2][:, t % 2, :],
                                           scalar=quarter_rs[:, t:t + 1], in1=gap[:, t, :], op0=ALU.mult, op1=ALU.mult)
        for q in range(2):
            nc.vector.scalar_tensor_tensor(out=gate_term[:, pairs[q], :], in0=s[:, pairs[q], :], scalar=1.0,
                                           in1=tb_gap[:, pairs[q], :], op0=ALU.subtract, op1=ALU.mult)
        for t in range(SLOTS):
            nc.vector.scalar_tensor_tensor(out=inner[:, t, :], in0=minus_th1[:, t, :],
                                           scalar=minus_half_rs[:, t:t + 1], in1=gate_term[:, t, :],
                                           op0=ALU.mult, op1=ALU.add)

        def finish_fo1(cols):
            nc.vector.scalar_tensor_tensor(out=fo1[:, :, cols], in0=s[:, :, cols], scalar=1.0, in1=inner[:, :, cols],
                                           op0=ALU.add, op1=ALU.mult)

        halves = [slice(0, HALF), slice(HALF, J)]
        third_quarter, last_quarter = slice(HALF, HALF + QUARTER), slice(HALF + QUARTER, J)
        fo1_grouped = [tile("fo1_grouped%d" % k, [P, SLOTS * HALF], BF16) for k in range(2)]
        y_grouped = [tile("y_grouped%d" % k, [P, SLOTS * HALF], BF16) for k in range(2)]
        y = [tile("y%d" % k, [P, SLOTS, HALF], F32) for k in range(2)]
        y_codes = tile("y_codes", [P, J], U32)
        y_scales = tile("y_scales", [P, J], U8)
        words_out = out_1[0].rearrange("p c r -> p (c r)").bitcast(I32)

        def in_half(cols):
            k = cols.start // HALF
            return k, slice(cols.start - k * HALF, cols.stop - k * HALF)

        def group_slots(copy, dst, cols, src):
            k, part = in_half(cols)
            out = dst[k][:, SLOTS * part.start:SLOTS * part.stop].rearrange("p (c i t) -> p c t i", i=4, t=SLOTS)
            copy(out, src.rearrange("p t (c i) -> p c t i", i=4))

        def group_fo1(copy, cols):
            group_slots(copy, fo1_grouped, cols, fo1[:, :, cols])

        def group_y(copy, cols):
            k, part = in_half(cols)
            group_slots(copy, y_grouped, cols, y[k][:, :, part])

        def last_layer(k):
            fo1_codes = tile("fo1_codes%d" % k, [P, HALF], U32)
            fo1_scales = tile("fo1_scales%d" % k, [P, HALF], U8)
            nc.vector.quantize_mx(out=fo1_codes[:].bitcast(FP8X4), scales=fo1_scales[:], in_=fo1_grouped[k][:])
            bank = psum.tile([P, SLOTS, HALF], F32, name="yo%d" % k, tag="a%d" % k)
            product(bank, "wor", all_slots, fo1_codes[:].bitcast(FP8X4), fo1_scales[:])
            return bank

        def add_residual(yo, cols):
            k, part = in_half(cols)
            nc.vector.tensor_tensor(y[k][:, :, part], yo[:, :, part], res_sb[:, :, cols], ALU.add)

        def store_y(k):
            nc.sync.dma_start(out=by_slot(out_0)[:, :, halves[k]], in_=y[k][:])

        def planes(k):
            cols = halves[k]
            nc.vector.quantize_mx(out=y_codes[:, cols].bitcast(FP8X4), scales=y_scales[:, cols], in_=y_grouped[k][:])
            nc.sync.dma_start(out=words_out[:, cols], in_=y_codes[:, cols].bitcast(I32))

        finish_fo1(halves[0])
        group_fo1(nc.scalar.copy, halves[0])
        quantize_weight("wor", all_slots)
        finish_fo1(third_quarter)
        group_fo1(nc.scalar.copy, third_quarter)
        finish_fo1(last_quarter)
        yo_first = last_layer(0)
        group_fo1(nc.vector.tensor_copy, last_quarter)
        yo_second = last_layer(1)
        add_residual(yo_first, halves[0])
        store_y(0)
        group_y(nc.scalar.copy, halves[0])
        add_residual(yo_second, third_quarter)
        add_residual(yo_second, last_quarter)
        store_y(1)
        group_y(nc.scalar.copy, third_quarter)
        planes(0)
        group_y(nc.vector.tensor_copy, last_quarter)
        planes(1)

        scale_rows = out_2[0].bitcast(I32)
        for quadrant, queue in enumerate((nc.scalar, nc.scalar, nc.scalar, nc.sync)):
            queue.dma_start(out=scale_rows[4 * quadrant:4 * quadrant + 4, :],
                            in_=y_scales[32 * quadrant:32 * quadrant + 4, :].bitcast(I32))
